import numpy as np
import ml_dtypes


def mxq(x, axis, fmt="e4m3"):
    dtype, down = {"e4m3": (ml_dtypes.float8_e4m3fn, 7), "e5m2": (ml_dtypes.float8_e5m2, 14)}[fmt]
    v = np.moveaxis(np.asarray(x, np.float32).astype(ml_dtypes.bfloat16).astype(np.float64), axis, -1)
    blocks = v.reshape(v.shape[:-1] + (-1, 32))
    amax = np.abs(blocks).max(-1, keepdims=True)
    byte = np.maximum(np.where(amax > 0, np.frexp(amax)[1] - 1 + 127, 0) - down, 1)
    scale = np.exp2(byte - 127.0)
    codes = (blocks / scale).astype(np.float32).astype(dtype).astype(np.float64)
    return np.moveaxis((codes * scale).reshape(v.shape), -1, axis)


WIDE = False


def mx_kscale(k):
    if not WIDE:
        return np.ones(k)
    levels = np.array([10, -10, 5, -5, 0])
    if k % 512:
        return np.exp2(np.random.permutation(np.resize(levels, k // 32))).repeat(32)
    a = np.empty((k // 512, 16))
    for p in range(k // 512):
        a[p, :8] = np.random.permutation(np.resize(levels, 8))
        for g in range(8):
            far = levels[np.abs(levels - a[p, g]) >= 10]
            a[p, g + 8] = far[np.random.randint(len(far))]
    return np.exp2(a.ravel()).repeat(32)


BF16 = ml_dtypes.bfloat16


def bf(x):
    return np.asarray(x, np.float32).astype(BF16)


def f64(x):
    return np.asarray(x).astype(np.float64)


E2M1 = np.array([0.0, 0.5, 1.0, 1.5, 2.0, 3.0, 4.0, 6.0, -0.0, -0.5, -1.0, -1.5, -2.0, -3.0, -4.0, -6.0])


def pack_weight(w, fmt):
    k, n = w.shape
    w = f64(bf(w)).reshape(k // 32, 32, n)
    amax = np.abs(w).max(1)
    if fmt == "e4m3":
        byte = np.frexp(amax)[1] - 1 + 127 - 7
    else:
        mant, ex = np.frexp(amax / 6.0)
        byte = np.where(mant > 0.5, ex, ex - 1) + 127
    byte = np.clip(np.where(amax > 0, byte, 1), 1, 254)
    scaled = (w * np.exp2(127.0 - byte)[:, None, :]).reshape(k, n).astype(np.float32)
    by_word = np.ascontiguousarray(scaled.reshape(k // 512, 128, 4, n).transpose(0, 1, 3, 2))
    if fmt == "e4m3":
        words = by_word.astype(ml_dtypes.float8_e4m3fn).view(np.uint8)
    else:
        c = by_word.astype(ml_dtypes.float4_e2m1fn).view(np.uint8) & 0xF
        words = c[..., 0::2] | (c[..., 1::2] << 4)
    return np.ascontiguousarray(words), np.ascontiguousarray(byte.astype(np.uint8).reshape(k // 512, 16, n))


def unpack_weight(words, scales, fmt):
    g, p, n, _ = words.shape
    if fmt == "e4m3":
        vals = np.ascontiguousarray(words).view(ml_dtypes.float8_e4m3fn).astype(np.float64)
    else:
        nib = np.empty((g, p, n, 4), np.uint8)
        nib[..., 0::2] = words & 0xF
        nib[..., 1::2] = words >> 4
        vals = E2M1[nib]
    vals = vals * np.repeat(np.exp2(scales.astype(np.float64) - 127.0), 8, axis=1)[..., None]
    return vals.transpose(0, 1, 3, 2).reshape(g * 512, n)
def pack4(w):
    words, scales = pack_weight(w, "e2m1")
    return words.reshape(words.shape[0], 128, -1), scales


def unpack4(words, scales):
    return unpack_weight(words.reshape(words.shape[0], 128, -1, 2), scales, "e2m1")


M, KF, KI, F, R = 1024, 1024, 2048, 1024, 512


def setup_inputs():
    s = mx_kscale(KF)
    u = mx_kscale(KI)
    t = mx_kscale(F)
    b2_words, b2_scales = pack4(np.random.standard_normal((KI, F)) / np.sqrt(KF + KI) / u[:, None])
    w_words, w_scales = pack4(np.random.standard_normal((F, R)) / np.sqrt(F) / t[:, None])
    return {"filler": bf(np.random.standard_normal((M, KF)) * s),
            "inter": bf(np.random.standard_normal((M, KI)) * u),
            "b1": bf(np.random.standard_normal((KF, F)) / np.sqrt(KF + KI) / s[:, None]),
            "b2_words": b2_words,
            "b2_scales": b2_scales,
            "gain": bf((1 + 0.1 * np.random.standard_normal(F)) * t),
            "w_words": w_words,
            "w_scales": w_scales,
            "e0": bf(0.4 * np.random.standard_normal(R))}


def reference(filler, inter, b1, b2_words, b2_scales, gain, w_words, w_scales, e0):
    c = ((mxq(f64(filler), 1, "e4m3") @ mxq(f64(b1), 0, "e4m3"))
         + (mxq(f64(inter), 1, "e4m3") @ unpack4(b2_words, b2_scales)))
    h = np.square(c) * f64(gain)
    return (mxq(h, 1, "e4m3") @ unpack4(w_words, w_scales)) + f64(e0)

@@ -1,0 +1,368 @@
+from contextlib import ExitStack
+
+import concourse.mybir as mybir
+from concourse.masks import make_identity
+
+M, KF, KI, F, R = 1024, 1024, 2048, 1024, 512
+FLOPS = 2 * M * (KF + KI) * F + 2 * M * F * R
+
+F32 = mybir.dt.float32
+BF16 = mybir.dt.bfloat16
+I32 = mybir.dt.int32
+U32 = mybir.dt.uint32
+U8 = mybir.dt.uint8
+FP8X4 = mybir.dt.float8_e4m3fn_x4
+FP4X4 = mybir.dt.float4_e2m1fn_x4
+ACT = mybir.ActivationFunctionType
+ALU = mybir.AluOpType
+
+P = 128
+HALF = 512
+TILES = M // P
+SORT_FROM = 2
+ACT_SORT = 1
+ACT_B1 = 0
+WARM = 0
+
+
+def tile_squared_projection_modulus_s3_kernel(
+    tc, filler, inter, b1, b2_words, b2_scales, gain, w_words, w_scales, e0, out
+):
+    nc = tc.nc
+    with ExitStack() as ctx:
+        keep = ctx.enter_context(tc.tile_pool(name="keep", bufs=1))
+        work = ctx.enter_context(tc.tile_pool(name="work", bufs=4))
+        psum = ctx.enter_context(tc.psum_pool(name="psum", bufs=1))
+        ctx.enter_context(tc.manual_schedule())
+
+        ident = keep.tile([P, P], F32, name="ident")
+        make_identity(nc, ident[:])
+        b2_plane = keep.tile([P, 4, F], U8, name="b2_plane", align_bytes=64)
+        w_plane = keep.tile([P, 2, R], U8, name="w_plane", align_bytes=64)
+
+        x_raw, x_words, x_q, b1_raw, b1_q, b2_half, acc, h_bf, h_q = {}, {}, {}, {}, {}, {}, {}, {}, {}
+        count = {"turn": 0}
+
+        def load_chunks(i, chunks):
+            t = keep.tile([P, 1024 * len(chunks)], BF16, name="x_raw_%d_%d" % (i, chunks[0]))
+            rows = slice(P * i, P * (i + 1))
+            if chunks[0] == 2:
+                src = filler[rows, :]
+            else:
+                src = inter[rows, 1024 * chunks[0] : 1024 * (chunks[-1] + 1)]
+            nc.sync.dma_start(out=t[:], in_=src)
+            for n, c in enumerate(chunks):
+                x_raw[i, c] = t[:, 1024 * n : 1024 * (n + 1)].bitcast(F32)
+
+        def load_b2(h):
+            t = keep.tile([P, 4, 2 * HALF], U8, name="b2_%d" % h, align_bytes=64)
+            src = b2_words[:, :, 2 * HALF * h : 2 * HALF * (h + 1)].rearrange("g p n -> p g n")
+            nc.sync.dma_start(out=t[:].bitcast(I32), in_=src.bitcast(I32))
+            b2_half[h] = t
+
+        def load_scales(engine, plane, scales):
+            for q in range(4):
+                src = scales[:, 4 * q : 4 * q + 4, :].rearrange("g r n -> r g n")
+                engine.dma_start(out=plane[32 * q : 32 * q + 4, :, :].bitcast(I32), in_=src.bitcast(I32))
+
+        def load_b1(g, h):
+            t = keep.tile([P, 4, HALF], BF16, name="b1_raw_%d_%d" % (g, h))
+            src = b1[512 * g : 512 * (g + 1), HALF * h : HALF * (h + 1)].rearrange("(p j) n -> p j n", j=4)
+            nc.sync.dma_start(out=t[:], in_=src)
+            b1_raw[g, h] = t
+
+        def turn_bank():
+            bank = psum.tile([P, 4, P], F32, name="turn_%d" % (count["turn"] % 4))
+            count["turn"] = count["turn"] + 1
+            return bank
+
+        def quantise(name, values):
+            width = values.shape[1] // 4
+            codes = keep.tile([P, width], U32, name=name + "_codes", align_bytes=64)
+            plane = keep.tile([P, width], U8, name=name + "_plane", align_bytes=64)
+            nc.vector.quantize_mx(out=codes[:].bitcast(FP8X4), scales=plane[:], in_=values)
+            return codes, plane
+
+        def b1_interleave(g, h, on_scalar):
+            t = work.tile([P, HALF, 4], BF16, name="b1_grouped", bufs=2, align_bytes=64)
+            dst = t[:].rearrange("p (c i) t -> p c t i", i=4)
+            src = b1_raw[g, h][:].rearrange("p t (c i) -> p c t i", i=4)
+            if on_scalar:
+                nc.scalar.copy(out=dst, in_=src)
+            else:
+                nc.vector.tensor_copy(out=dst, in_=src)
+            b1_raw[g, h] = t
+
+        def b1_quantise(g, h):
+            b1_q[g, h] = quantise("b1_%d_%d" % (g, h), b1_raw[g, h][:].rearrange("p n t -> p (n t)"))
+
+        def sort_words(i, c, on_scalar=False):
+            t = work.tile([P, 2, 2, P], F32, name="x_sorted", bufs=6)
+            src = x_raw[i, c].rearrange("p (g q u) -> p g u q", g=2, u=2)
+            if on_scalar:
+                nc.scalar.copy(out=t[:], in_=src)
+            else:
+                nc.vector.tensor_copy(out=t[:], in_=src)
+            x_words[i, c] = t
+
+        def turn_x(i, c):
+            bank = turn_bank()
+            for g in range(2):
+                for u in range(2):
+                    if (i, c) in x_words:
+                        src = x_words[i, c][:, g, u, :]
+                    else:
+                        src = x_raw[i, c][:, 256 * g + u : 256 * (g + 1) : 2]
+                    nc.tensor.transpose(bank[:, 2 * g + u, :], src, ident[:])
+            return bank
+
+        def turn_h(units):
+            bank = turn_bank()
+            for n, unit in enumerate(units):
+                words = h_bf[unit][:].bitcast(F32)
+                for u in range(2):
+                    nc.tensor.transpose(bank[:, 2 * n + u, :], words[:, P * u : P * (u + 1)], ident[:])
+            return bank
+
+        def empty_turn(bank, passes):
+            t = work.tile([P, passes * HALF], BF16, name="turned", bufs=6, align_bytes=64)
+            nc.scalar.copy(
+                out=t[:].bitcast(F32).rearrange("p (g m u) -> p g m u", g=passes, u=2),
+                in_=bank[:, 0 : 2 * passes, :].rearrange("p (g u) m -> p g m u", u=2),
+            )
+            return t
+
+        def mx(bank, lhs, n, rhs, rhs_scale, start, stop):
+            cols = slice(P * n, P * (n + 1))
+            nc.tensor.matmul_mx(
+                out=bank[:], lhsT=lhs[0][:, cols].bitcast(FP8X4), lhsT_scale=lhs[1][:, cols],
+                rhs=rhs, rhs_scale=rhs_scale, start=start, stop=stop,
+            )
+
+        def mm_inter(i, h, slot):
+            bank = psum.tile([P, HALF], F32, name="acc_%d" % slot)
+            acc[i, h] = bank
+            for g in range(4):
+                mx(bank, x_q[i, g // 2], g % 2, b2_half[h][:, g, :].bitcast(FP4X4),
+                   b2_plane[:, g, HALF * h : HALF * (h + 1)], g == 0, False)
+
+        def mm_filler(i, h):
+            for g in range(2):
+                codes, plane = b1_q[g, h]
+                mx(acc[i, h], x_q[i, 2], g, codes[:].bitcast(FP8X4), plane[:], False, g == 1)
+
+        def mm_out(i, slot, halves=(0, 1)):
+            if 0 in halves:
+                acc[i] = psum.tile([P, R], F32, name="acc_%d" % slot)
+            bank = acc[i]
+            for h in halves:
+                q, n = h_q[i, h]
+                mx(bank, q, n, w_sb[:, h, :].bitcast(FP4X4), w_plane[:, h, :], h == 0, h == 1)
+
+        def square_gain(i, h, pieces=1):
+            t = work.tile([P, HALF], BF16, name="h_bf", bufs=8)
+            h_bf[i, h] = t
+            n = 2 // pieces
+            for u in range(0, 2, n):
+                sq = work.tile([P, n, P, 2], F32, name="square")
+                src = acc[i, h][:].rearrange("p (q u e) -> p u q e", u=2, e=2)
+                nc.scalar.activation(out=sq[:], in_=src[:, u : u + n, :, :], func=ACT.Square)
+                cols = slice(256 * u, 256 * (u + n))
+                nc.vector.tensor_tensor(
+                    out=t[:, cols], in0=sq[:].rearrange("p u q e -> p (u q e)"),
+                    in1=gain_sb[:, HALF * h + 256 * u : HALF * h + 256 * (u + n)], op=ALU.mult,
+                )
+
+        def finish(i, pieces=1):
+            width = R // pieces
+            for n in range(pieces):
+                cols = slice(width * n, width * (n + 1))
+                t = work.tile([P, width], F32, name="result")
+                nc.vector.tensor_tensor(out=t[:], in0=acc[i][:, cols], in1=e0_sb[:, cols], op=ALU.add)
+                nc.sync.dma_start(out=out[P * i : P * (i + 1), cols], in_=t[:])
+
+        def turn_run(xs, hs, between=None):
+            banks = [turn_x(i, c) for i, c in xs]
+            hbanks = [turn_h(units) for units in hs]
+            staged = [empty_turn(bank, 2) for bank in banks]
+            hstaged = [empty_turn(bank, len(units)) for units, bank in zip(hs, hbanks)]
+            if between:
+                between()
+            for (i, c), t in zip(xs, staged):
+                x_q[i, c] = quantise("x_%d_%d" % (i, c), t[:])
+            for units, t in zip(hs, hstaged):
+                q = quantise("h_%d_%d" % units[0], t[:])
+                for n, unit in enumerate(units):
+                    h_q[unit] = (q, n)
+
+        gain_col = keep.tile([P, 2, 4], BF16, name="gain_col")
+        e0_col = keep.tile([P, 4], BF16, name="e0_col")
+        w_sb = keep.tile([P, 2, 2 * R], U8, name="w_sb", align_bytes=64)
+        gain_sb = keep.tile([P, F], BF16, name="gain_sb")
+        e0_sb = keep.tile([P, R], BF16, name="e0_sb")
+
+        def load_vectors(engine):
+            engine.dma_start(out=gain_col[:], in_=gain.rearrange("(g p j) -> p g j", g=2, j=4))
+            engine.dma_start(out=e0_col[:], in_=e0.rearrange("(p j) -> p j", j=4))
+
+        def load_w():
+            nc.sync.dma_start(out=w_sb[:].bitcast(I32), in_=w_words.rearrange("g p n -> p g n").bitcast(I32))
+            load_scales(nc.sync, w_plane, w_scales)
+
+        def spread_gain():
+            bank = turn_bank()
+            words = gain_col[:].rearrange("p g j -> p (g j)").bitcast(F32)
+            for n in range(4):
+                nc.tensor.transpose(bank[:, n, :], words[:, n : n + 1].to_broadcast([P, P]), ident[:])
+            nc.scalar.copy(out=gain_sb[:].bitcast(F32), in_=bank[:].rearrange("p n m -> p (n m)"))
+
+        def spread_e0():
+            bank2 = turn_bank()
+            words = e0_col[:].bitcast(F32)
+            for n in range(2):
+                nc.tensor.transpose(bank2[:, n, :], words[:, n : n + 1].to_broadcast([P, P]), ident[:])
+            nc.scalar.copy(
+                out=e0_sb[:].bitcast(F32).rearrange("p (m u) -> p m u", u=2),
+                in_=bank2[:, 0:2, :].rearrange("p u m -> p m u"),
+            )
+
+        def sort_tile(i, chunks, scalar_chunks=()):
+            for c in chunks:
+                sort_words(i, c, c in scalar_chunks)
+
+        def mm_unit(i, h, slot):
+            mm_inter(i, h, slot)
+            mm_filler(i, h)
+
+        def warm(n):
+            bank = psum.tile([P, 4, P], F32, name="acc_3")
+            for rep in range(n):
+                nc.tensor.matmul_mx(out=bank[:, rep % 4, :], lhsT=wq[0][:].bitcast(FP8X4), lhsT_scale=wq[1][:],
+                                    rhs=wq[0][:].bitcast(FP8X4), rhs_scale=wq[1][:], start=True, stop=True)
+
+        def both(i):
+            return [(i, 0), (i, 1)]
+
+        table_warm = keep.tile([P, 1], F32, name="table_warm")
+
+        if WARM:
+            wz = keep.tile([P, 512], BF16, name="wz", align_bytes=64)
+            nc.vector.memset(wz[:], 1.0)
+        nc.vector.memset(b2_plane[:].bitcast(U32), 0)
+        if WARM:
+            wq = quantise("warm", wz[:])
+        nc.vector.memset(w_plane[:].bitcast(U32), 0)
+        load_vectors(nc.gpsimd)
+
+        SC = (2,)
+        load_chunks(0, [0])
+        load_chunks(0, [1])
+        load_scales(nc.scalar, b2_plane, b2_scales)
+        nc.scalar.activation(out=table_warm[:], in_=ident[:, 0:1], func=ACT.Square)
+        load_chunks(1, [0, 1])
+        load_b2(0)
+        load_chunks(2, [0, 1])
+        load_b1(0, 0)
+        load_chunks(0, [2])
+        load_b1(1, 0)
+        load_chunks(1, [2])
+        load_chunks(3, [0, 1])
+        load_b2(1)
+        load_chunks(2, [2])
+        load_chunks(3, [2])
+        load_b1(0, 1)
+        load_b1(1, 1)
+        load_chunks(4, [0, 1])
+        load_chunks(4, [2])
+        load_w()
+        for i in range(5, TILES):
+            load_chunks(i, [0, 1])
+            load_chunks(i, [2])
+
+        if WARM:
+            warm(WARM)
+        sort_tile(0, [0, 1])
+        turn_run([(0, 0), (0, 1)], [])
+        spread_gain()
+        spread_e0()
+        if WARM:
+            warm(WARM)
+        sort_tile(1, [0, 1])
+        turn_run([(1, 0), (1, 1)], [])
+        sort_tile(2, [0, 1])
+        mm_inter(0, 0, 0)
+        turn_run([(2, 0), (2, 1)], [], lambda: b1_interleave(0, 0, False))
+        sort_words(0, 2, True)
+        mm_inter(1, 0, 1)
+        turn_run([(0, 2)], [], lambda: b1_quantise(0, 0))
+        b1_interleave(1, 0, False)
+        sort_words(1, 2, True)
+        mm_inter(2, 0, 2)
+        sort_words(3, 0, True)
+        sort_words(3, 1, False)
+        b1_quantise(1, 0)
+        turn_run([(1, 2), (3, 0), (3, 1)], [])
+        mm_filler(0, 0)
+        mm_filler(1, 0)
+        sort_words(2, 2, False)
+        sort_words(3, 2, False)
+        square_gain(0, 0)
+        square_gain(1, 0)
+        mm_inter(3, 0, 3)
+        turn_run([(2, 2), (3, 2)], [], lambda: b1_interleave(0, 1, False))
+        mm_inter(0, 1, 0)
+        mm_inter(1, 1, 1)
+        b1_quantise(0, 1)
+        b1_interleave(1, 1, False)
+        sort_words(4, 0, True)
+        sort_words(4, 1, True)
+        mm_filler(2, 0)
+        mm_filler(3, 0)
+        b1_quantise(1, 1)
+        sort_words(4, 2, False)
+        square_gain(2, 0)
+        square_gain(3, 0)
+        turn_run([(4, 0), (4, 1), (4, 2)], [[(0, 0), (1, 0)]])
+        mm_inter(2, 1, 2)
+        mm_filler(0, 1)
+        mm_filler(1, 1)
+        square_gain(0, 1)
+        square_gain(1, 1)
+        mm_inter(3, 1, 3)
+        mm_filler(2, 1)
+        mm_filler(3, 1)
+        sort_tile(5, [0, 1], ())
+        square_gain(2, 1)
+        square_gain(3, 1)
+
+        mm_unit(4, 0, 0)
+        turn_run([(5, 0), (5, 1)], [[(0, 1), (1, 1)], [(2, 0), (3, 0)]])
+        sort_words(5, 2, False)
+        square_gain(4, 0)
+        mm_unit(4, 1, 1)
+        mm_out(0, 2)
+        mm_out(1, 3)
+        turn_run([(5, 2)], [[(2, 1), (3, 1)]], lambda: finish(0))
+        finish(1)
+        square_gain(4, 1)
+        sort_tile(6, [0, 1, 2], SC)
+        for i in range(5, TILES):
+            mm_unit(i, 0, 0)
+            if i == 5:
+                mm_out(2, 2)
+                mm_out(3, 3)
+                finish(2)
+            else:
+                mm_out(i - 2, 2 + i % 2)
+            square_gain(i, 0)
+            turn_run([(i + 1, c) for c in range(3)] if i + 1 < TILES else [], [both(i - 1)], lambda: finish(i - 2))
+            mm_unit(i, 1, 1)
+            if i + 2 < TILES:
+                sort_tile(i + 2, [0, 1, 2], SC)
+            square_gain(i, 1, 2 if i == 7 else 1)
+        turn_run([], [[(7, 0)]])
+        mm_out(6, 2)
+        mm_out(7, 0, (0,))
+        turn_run([], [[(7, 1)]], lambda: finish(6))
+        mm_out(7, 0, (1,))
+        finish(7, 2)

@@ -13,16 +13,17 @@ U32 = mybir.dt.uint32
 U8 = mybir.dt.uint8
 FP8X4 = mybir.dt.float8_e4m3fn_x4
 FP4X4 = mybir.dt.float4_e2m1fn_x4
-ACT = mybir.ActivationFunctionType
+SQUARE = mybir.ActivationFunctionType.Square
 ALU = mybir.AluOpType
 
 P = 128
+PASS = 512
 HALF = 512
+CHUNK = 2 * PASS
+FILLER = 2
 TILES = M // P
-SORT_FROM = 2
-ACT_SORT = 1
-ACT_B1 = 0
-WARM = 0
+HEAD = 3
+WARM_FIRST, WARM_SECOND = 10, 6
 
 
 def tile_squared_projection_modulus_s3_kernel(
@@ -35,334 +36,347 @@ def tile_squared_projection_modulus_s3_kernel(
         psum = ctx.enter_context(tc.psum_pool(name="psum", bufs=1))
         ctx.enter_context(tc.manual_schedule())
 
-        ident = keep.tile([P, P], F32, name="ident")
-        make_identity(nc, ident[:])
-        b2_plane = keep.tile([P, 4, F], U8, name="b2_plane", align_bytes=64)
-        w_plane = keep.tile([P, 2, R], U8, name="w_plane", align_bytes=64)
+        raw = {}
+        pairs = {}
+        stationary = {}
+        moving = {}
+        b1_stage = {}
+        sums = {}
 
-        x_raw, x_words, x_q, b1_raw, b1_q, b2_half, acc, h_bf, h_q = {}, {}, {}, {}, {}, {}, {}, {}, {}
-        count = {"turn": 0}
+        def bank_tile(bank, shape):
+            return psum.tile(shape, F32, name="bank_%d" % bank)
 
-        def load_chunks(i, chunks):
-            t = keep.tile([P, 1024 * len(chunks)], BF16, name="x_raw_%d_%d" % (i, chunks[0]))
+        def load_samples(i, chunks):
+            staged = keep.tile([P, CHUNK * len(chunks)], BF16, name="raw_%d_%d" % (i, chunks[0]))
             rows = slice(P * i, P * (i + 1))
-            if chunks[0] == 2:
-                src = filler[rows, :]
+            if chunks[0] == FILLER:
+                source = filler[rows, :]
             else:
-                src = inter[rows, 1024 * chunks[0] : 1024 * (chunks[-1] + 1)]
-            nc.sync.dma_start(out=t[:], in_=src)
+                source = inter[rows, CHUNK * chunks[0] : CHUNK * (chunks[-1] + 1)]
+            nc.sync.dma_start(out=staged[:], in_=source)
             for n, c in enumerate(chunks):
-                x_raw[i, c] = t[:, 1024 * n : 1024 * (n + 1)].bitcast(F32)
+                raw[i, c] = staged[:, CHUNK * n : CHUNK * (n + 1)].bitcast(F32)
 
-        def load_b2(h):
-            t = keep.tile([P, 4, 2 * HALF], U8, name="b2_%d" % h, align_bytes=64)
-            src = b2_words[:, :, 2 * HALF * h : 2 * HALF * (h + 1)].rearrange("g p n -> p g n")
-            nc.sync.dma_start(out=t[:].bitcast(I32), in_=src.bitcast(I32))
-            b2_half[h] = t
+        def new_plane(name, width):
+            plane = keep.tile([P, 2, width], U8, name=name, align_bytes=64)
+            nc.vector.memset(plane[:].bitcast(U32), 0)
+            return plane
 
-        def load_scales(engine, plane, scales):
+        def load_fp4(name, words, scales, plane):
             for q in range(4):
-                src = scales[:, 4 * q : 4 * q + 4, :].rearrange("g r n -> r g n")
-                engine.dma_start(out=plane[32 * q : 32 * q + 4, :, :].bitcast(I32), in_=src.bitcast(I32))
+                rows = scales[:, 4 * q : 4 * q + 4, :].rearrange("g r n -> r g n")
+                nc.sync.dma_start(out=plane[32 * q : 32 * q + 4, :, :].bitcast(I32), in_=rows.bitcast(I32))
+            codes = keep.tile([P, 2, words.shape[2]], U8, name=name, align_bytes=64)
+            nc.sync.dma_start(out=codes[:].bitcast(I32), in_=words.rearrange("g p n -> p g n").bitcast(I32))
+            return codes
+
+        def load_b2(c):
+            passes = slice(2 * c, 2 * c + 2)
+            codes = load_fp4("b2_%d" % c, b2_words[passes], b2_scales[passes], b2_planes[c])
+            for g in range(2):
+                for h in range(2):
+                    moving[c, g, h] = (
+                        codes[:, g, 2 * HALF * h : 2 * HALF * (h + 1)].bitcast(FP4X4),
+                        b2_planes[c][:, g, HALF * h : HALF * (h + 1)],
+                    )
+
+        def load_w():
+            codes = load_fp4("w", w_words, w_scales, w_plane)
+            for h in range(2):
+                moving["w", h] = (codes[:, h, :].bitcast(FP4X4), w_plane[:, h, :])
 
         def load_b1(g, h):
-            t = keep.tile([P, 4, HALF], BF16, name="b1_raw_%d_%d" % (g, h))
-            src = b1[512 * g : 512 * (g + 1), HALF * h : HALF * (h + 1)].rearrange("(p j) n -> p j n", j=4)
-            nc.sync.dma_start(out=t[:], in_=src)
-            b1_raw[g, h] = t
+            staged = keep.tile([P, 4, HALF], BF16, name="b1_rows_%d_%d" % (g, h))
+            rows = b1[PASS * g : PASS * (g + 1), HALF * h : HALF * (h + 1)]
+            nc.sync.dma_start(out=staged[:], in_=rows.rearrange("(p t) n -> p t n", t=4))
+            b1_stage[g, h] = staged
 
-        def turn_bank():
-            bank = psum.tile([P, 4, P], F32, name="turn_%d" % (count["turn"] % 4))
-            count["turn"] = count["turn"] + 1
-            return bank
+        def load_vector(name, vector):
+            run = vector.shape[0] // P
+            staged = keep.tile([P, run], BF16, name=name)
+            nc.sync.dma_start(out=staged[:], in_=vector.rearrange("(p j) -> p j", j=run))
+            return staged
 
         def quantise(name, values):
             width = values.shape[1] // 4
-            codes = keep.tile([P, width], U32, name=name + "_codes", align_bytes=64)
+            words = keep.tile([P, width], U32, name=name + "_words", align_bytes=64)
             plane = keep.tile([P, width], U8, name=name + "_plane", align_bytes=64)
-            nc.vector.quantize_mx(out=codes[:].bitcast(FP8X4), scales=plane[:], in_=values)
-            return codes, plane
+            nc.vector.quantize_mx(out=words[:].bitcast(FP8X4), scales=plane[:], in_=values)
+            return words, plane
 
-        def b1_interleave(g, h, on_scalar):
-            t = work.tile([P, HALF, 4], BF16, name="b1_grouped", bufs=2, align_bytes=64)
-            dst = t[:].rearrange("p (c i) t -> p c t i", i=4)
-            src = b1_raw[g, h][:].rearrange("p t (c i) -> p c t i", i=4)
-            if on_scalar:
-                nc.scalar.copy(out=dst, in_=src)
-            else:
-                nc.vector.tensor_copy(out=dst, in_=src)
-            b1_raw[g, h] = t
-
-        def b1_quantise(g, h):
-            b1_q[g, h] = quantise("b1_%d_%d" % (g, h), b1_raw[g, h][:].rearrange("p n t -> p (n t)"))
-
-        def sort_words(i, c, on_scalar=False):
-            t = work.tile([P, 2, 2, P], F32, name="x_sorted", bufs=6)
-            src = x_raw[i, c].rearrange("p (g q u) -> p g u q", g=2, u=2)
-            if on_scalar:
-                nc.scalar.copy(out=t[:], in_=src)
-            else:
-                nc.vector.tensor_copy(out=t[:], in_=src)
-            x_words[i, c] = t
-
-        def turn_x(i, c):
-            bank = turn_bank()
-            for g in range(2):
-                for u in range(2):
-                    if (i, c) in x_words:
-                        src = x_words[i, c][:, g, u, :]
-                    else:
-                        src = x_raw[i, c][:, 256 * g + u : 256 * (g + 1) : 2]
-                    nc.tensor.transpose(bank[:, 2 * g + u, :], src, ident[:])
-            return bank
-
-        def turn_h(units):
-            bank = turn_bank()
-            for n, unit in enumerate(units):
-                words = h_bf[unit][:].bitcast(F32)
-                for u in range(2):
-                    nc.tensor.transpose(bank[:, 2 * n + u, :], words[:, P * u : P * (u + 1)], ident[:])
-            return bank
-
-        def empty_turn(bank, passes):
-            t = work.tile([P, passes * HALF], BF16, name="turned", bufs=6, align_bytes=64)
-            nc.scalar.copy(
-                out=t[:].bitcast(F32).rearrange("p (g m u) -> p g m u", g=passes, u=2),
-                in_=bank[:, 0 : 2 * passes, :].rearrange("p (g u) m -> p g m u", u=2),
+        def interleave_b1(g, h):
+            grouped = work.tile([P, HALF, 4], BF16, name="b1_grouped", bufs=2, align_bytes=64)
+            nc.vector.tensor_copy(
+                out=grouped[:].rearrange("p (c i) t -> p c t i", i=4),
+                in_=b1_stage[g, h][:].rearrange("p t (c i) -> p c t i", i=4),
             )
-            return t
+            b1_stage[g, h] = grouped
 
-        def mx(bank, lhs, n, rhs, rhs_scale, start, stop):
-            cols = slice(P * n, P * (n + 1))
-            nc.tensor.matmul_mx(
-                out=bank[:], lhsT=lhs[0][:, cols].bitcast(FP8X4), lhsT_scale=lhs[1][:, cols],
-                rhs=rhs, rhs_scale=rhs_scale, start=start, stop=stop,
+        def quantise_b1(g, h):
+            words, plane = quantise("b1_%d_%d" % (g, h), b1_stage[g, h][:].rearrange("p n t -> p (n t)"))
+            moving[FILLER, g, h] = (words[:].bitcast(FP8X4), plane[:])
+
+        def sort_pairs(i, c, copy):
+            sorted_pairs = work.tile([P, 2, 2, P], F32, name="sorted_pairs", bufs=6)
+            copy(
+                out=sorted_pairs[:].rearrange("s u g (b i) -> s (g b) u i", i=4),
+                in_=raw[i, c].rearrange("s (b i u) -> s b u i", i=4, u=2),
             )
+            pairs[i, c] = sorted_pairs[:].rearrange("s u g p -> s g u p")
 
-        def mm_inter(i, h, slot):
-            bank = psum.tile([P, HALF], F32, name="acc_%d" % slot)
-            acc[i, h] = bank
-            for g in range(4):
-                mx(bank, x_q[i, g // 2], g % 2, b2_half[h][:, g, :].bitcast(FP4X4),
-                   b2_plane[:, g, HALF * h : HALF * (h + 1)], g == 0, False)
-
-        def mm_filler(i, h):
-            for g in range(2):
-                codes, plane = b1_q[g, h]
-                mx(acc[i, h], x_q[i, 2], g, codes[:].bitcast(FP8X4), plane[:], False, g == 1)
-
-        def mm_out(i, slot, halves=(0, 1)):
-            if 0 in halves:
-                acc[i] = psum.tile([P, R], F32, name="acc_%d" % slot)
-            bank = acc[i]
-            for h in halves:
-                q, n = h_q[i, h]
-                mx(bank, q, n, w_sb[:, h, :].bitcast(FP4X4), w_plane[:, h, :], h == 0, h == 1)
-
-        def square_gain(i, h, pieces=1):
-            t = work.tile([P, HALF], BF16, name="h_bf", bufs=8)
-            h_bf[i, h] = t
-            n = 2 // pieces
-            for u in range(0, 2, n):
-                sq = work.tile([P, n, P, 2], F32, name="square")
-                src = acc[i, h][:].rearrange("p (q u e) -> p u q e", u=2, e=2)
-                nc.scalar.activation(out=sq[:], in_=src[:, u : u + n, :, :], func=ACT.Square)
-                cols = slice(256 * u, 256 * (u + n))
-                nc.vector.tensor_tensor(
-                    out=t[:, cols], in0=sq[:].rearrange("p u q e -> p (u q e)"),
-                    in1=gain_sb[:, HALF * h + 256 * u : HALF * h + 256 * (u + n)], op=ALU.mult,
+        def turn(*jobs):
+            turned = []
+            banks = []
+            for bank, passes in jobs:
+                tile = bank_tile(bank, [P, 2, 2, P])
+                for n, (key, g) in enumerate(passes):
+                    for u in range(2):
+                        nc.tensor.transpose(tile[:, n, u, :], pairs[key][:, g, u, :], identity[:])
+                banks.append(tile)
+            for (bank, passes), tile in zip(jobs, banks):
+                values = work.tile([P, len(passes) * PASS], BF16, name="turned", bufs=6, align_bytes=64)
+                nc.scalar.copy(
+                    out=values[:].bitcast(F32).rearrange("p (n s u) -> p n s u", n=len(passes), u=2),
+                    in_=tile[:, 0 : len(passes), :, :].rearrange("p n u s -> p n s u"),
                 )
+                turned.append((passes, values))
+            return turned
+
+        def quantise_turned(turned):
+            for passes, values in turned:
+                name = "_".join(str(part) for part in passes[0][0])
+                words, plane = quantise("x_" + name, values[:])
+                for n, (key, g) in enumerate(passes):
+                    stationary[key, g] = (words[:, P * n : P * (n + 1)], plane[:, P * n : P * (n + 1)])
+
+        def chunk(bank, i, c):
+            return bank, [((i, c), 0), ((i, c), 1)]
+
+        def halves(bank, *units):
+            return bank, [((i, "h", h), 0) for i, h in units]
+
+        def spread(bank, staged, write, read):
+            words = staged[:].bitcast(F32)
+            count = words.shape[1]
+            tile = bank_tile(bank, [P, count, P])
+            for n in range(count):
+                nc.tensor.transpose(tile[:, n, :], words[:, n : n + 1].to_broadcast([P, P]), identity[:])
+            nc.scalar.copy(out=write, in_=read(tile[:]))
+
+        def spread_gain(bank):
+            spread(
+                bank, gain_runs,
+                gain_rows[:].bitcast(F32).rearrange("s (h u j v) -> s h u j v", h=2, u=2, v=2),
+                lambda tile: tile.rearrange("s (v u) (h j) -> s h u j v", u=2, h=2),
+            )
+
+        def spread_e0(bank):
+            spread(
+                bank, e0_runs,
+                e0_rows[:].bitcast(F32).rearrange("s (j n) -> s j n", n=2),
+                lambda tile: tile.rearrange("s n j -> s j n"),
+            )
+
+        def mx_pass(result, lhs, rhs, start, stop):
+            nc.tensor.matmul_mx(
+                out=result, lhsT=lhs[0].bitcast(FP8X4), lhsT_scale=lhs[1], rhs=rhs[0], rhs_scale=rhs[1],
+                start=start, stop=stop,
+            )
+
+        def project(i, h, chunks, bank=None, passes=(0, 1)):
+            if bank is not None:
+                sums[i, h] = bank_tile(bank, [P, HALF])
+            for c in chunks:
+                for g in passes:
+                    first, last = (c, g) == (0, 0), (c, g) == (FILLER, 1)
+                    mx_pass(sums[i, h][:], stationary[(i, c), g], moving[c, g, h], first, last)
+
+        def project_both(i, c):
+            for h in range(2):
+                project(i, h, [c], bank=2 * i + h if c == 0 else None)
+
+        def square_and_gain(i, h, pieces=1):
+            rounded = work.tile([P, HALF], BF16, name="rounded", bufs=8)
+            source = sums[i, h][:].rearrange("s (p u e) -> s u p e", u=2, e=2)
+            step = 2 // pieces
+            for u in range(0, 2, step):
+                squares = work.tile([P, step, P, 2], F32, name="squares")
+                nc.scalar.activation(out=squares[:], in_=source[:, u : u + step, :, :], func=SQUARE)
+                first, width = 2 * P * u, 2 * P * step
+                nc.vector.tensor_tensor(
+                    out=rounded[:, first : first + width],
+                    in0=squares[:].rearrange("s u p e -> s (u p e)"),
+                    in1=gain_rows[:, HALF * h + first : HALF * h + first + width],
+                    op=ALU.mult,
+                )
+            pairs[i, "h", h] = rounded[:].bitcast(F32).rearrange("s (g u p) -> s g u p", g=1, u=2)
+
+        def modulus(i, bank):
+            sums[i] = bank_tile(bank, [P, R])
+            for h in range(2):
+                mx_pass(sums[i][:], stationary[(i, "h", h), 0], moving["w", h], h == 0, h == 1)
 
         def finish(i, pieces=1):
             width = R // pieces
             for n in range(pieces):
                 cols = slice(width * n, width * (n + 1))
-                t = work.tile([P, width], F32, name="result")
-                nc.vector.tensor_tensor(out=t[:], in0=acc[i][:, cols], in1=e0_sb[:, cols], op=ALU.add)
-                nc.sync.dma_start(out=out[P * i : P * (i + 1), cols], in_=t[:])
+                result = work.tile([P, width], F32, name="result")
+                nc.vector.tensor_tensor(out=result[:], in0=sums[i][:, cols], in1=e0_rows[:, cols], op=ALU.add)
+                nc.sync.dma_start(out=out[P * i : P * (i + 1), cols], in_=result[:])
 
-        def turn_run(xs, hs, between=None):
-            banks = [turn_x(i, c) for i, c in xs]
-            hbanks = [turn_h(units) for units in hs]
-            staged = [empty_turn(bank, 2) for bank in banks]
-            hstaged = [empty_turn(bank, len(units)) for units, bank in zip(hs, hbanks)]
-            if between:
-                between()
-            for (i, c), t in zip(xs, staged):
-                x_q[i, c] = quantise("x_%d_%d" % (i, c), t[:])
-            for units, t in zip(hs, hstaged):
-                q = quantise("h_%d_%d" % units[0], t[:])
-                for n, unit in enumerate(units):
-                    h_q[unit] = (q, n)
+        def warm_up(passes):
+            tile = bank_tile(5, [P, 4, P])
+            for n in range(passes):
+                mx_pass(tile[:, n % 4, :], warm, (warm[0].bitcast(FP8X4), warm[1]), True, True)
 
-        gain_col = keep.tile([P, 2, 4], BF16, name="gain_col")
-        e0_col = keep.tile([P, 4], BF16, name="e0_col")
-        w_sb = keep.tile([P, 2, 2 * R], U8, name="w_sb", align_bytes=64)
-        gain_sb = keep.tile([P, F], BF16, name="gain_sb")
-        e0_sb = keep.tile([P, R], BF16, name="e0_sb")
+        on_vector, on_scalar = nc.vector.tensor_copy, nc.scalar.copy
+        inter_chunks = [0, 1]
+        all_chunks = [0, 1, FILLER]
 
-        def load_vectors(engine):
-            engine.dma_start(out=gain_col[:], in_=gain.rearrange("(g p j) -> p g j", g=2, j=4))
-            engine.dma_start(out=e0_col[:], in_=e0.rearrange("(p j) -> p j", j=4))
+        identity = keep.tile([P, P], F32, name="identity")
+        make_identity(nc, identity[:])
+        gain_rows = keep.tile([P, F], BF16, name="gain_rows")
+        e0_rows = keep.tile([P, R], BF16, name="e0_rows")
 
-        def load_w():
-            nc.sync.dma_start(out=w_sb[:].bitcast(I32), in_=w_words.rearrange("g p n -> p g n").bitcast(I32))
-            load_scales(nc.sync, w_plane, w_scales)
-
-        def spread_gain():
-            bank = turn_bank()
-            words = gain_col[:].rearrange("p g j -> p (g j)").bitcast(F32)
-            for n in range(4):
-                nc.tensor.transpose(bank[:, n, :], words[:, n : n + 1].to_broadcast([P, P]), ident[:])
-            nc.scalar.copy(out=gain_sb[:].bitcast(F32), in_=bank[:].rearrange("p n m -> p (n m)"))
-
-        def spread_e0():
-            bank2 = turn_bank()
-            words = e0_col[:].bitcast(F32)
-            for n in range(2):
-                nc.tensor.transpose(bank2[:, n, :], words[:, n : n + 1].to_broadcast([P, P]), ident[:])
-            nc.scalar.copy(
-                out=e0_sb[:].bitcast(F32).rearrange("p (m u) -> p m u", u=2),
-                in_=bank2[:, 0:2, :].rearrange("p u m -> p m u"),
-            )
-
-        def sort_tile(i, chunks, scalar_chunks=()):
-            for c in chunks:
-                sort_words(i, c, c in scalar_chunks)
-
-        def mm_unit(i, h, slot):
-            mm_inter(i, h, slot)
-            mm_filler(i, h)
-
-        def warm(n):
-            bank = psum.tile([P, 4, P], F32, name="acc_3")
-            for rep in range(n):
-                nc.tensor.matmul_mx(out=bank[:, rep % 4, :], lhsT=wq[0][:].bitcast(FP8X4), lhsT_scale=wq[1][:],
-                                    rhs=wq[0][:].bitcast(FP8X4), rhs_scale=wq[1][:], start=True, stop=True)
-
-        def both(i):
-            return [(i, 0), (i, 1)]
-
+        b2_planes = [new_plane("b2_plane_0", F)]
+        ones = keep.tile([P, PASS], BF16, name="ones", align_bytes=64)
+        nc.vector.memset(ones[:], 1.0)
+        warm_words, warm_plane = quantise("warm", ones[:])
+        warm = (warm_words[:], warm_plane[:])
+        b2_planes.append(new_plane("b2_plane_1", F))
+        w_plane = new_plane("w_plane", R)
         table_warm = keep.tile([P, 1], F32, name="table_warm")
+        nc.scalar.activation(out=table_warm[:], in_=identity[:, 0:1], func=SQUARE)
 
-        if WARM:
-            wz = keep.tile([P, 512], BF16, name="wz", align_bytes=64)
-            nc.vector.memset(wz[:], 1.0)
-        nc.vector.memset(b2_plane[:].bitcast(U32), 0)
-        if WARM:
-            wq = quantise("warm", wz[:])
-        nc.vector.memset(w_plane[:].bitcast(U32), 0)
-        load_vectors(nc.gpsimd)
-
-        SC = (2,)
-        load_chunks(0, [0])
-        load_chunks(0, [1])
-        load_scales(nc.scalar, b2_plane, b2_scales)
-        nc.scalar.activation(out=table_warm[:], in_=ident[:, 0:1], func=ACT.Square)
-        load_chunks(1, [0, 1])
+        head = range(HEAD)
+        for i in head:
+            load_samples(i, [0])
         load_b2(0)
-        load_chunks(2, [0, 1])
+        for i in head:
+            load_samples(i, [1])
         load_b1(0, 0)
-        load_chunks(0, [2])
-        load_b1(1, 0)
-        load_chunks(1, [2])
-        load_chunks(3, [0, 1])
+        gain_runs = load_vector("gain_runs", gain)
         load_b2(1)
-        load_chunks(2, [2])
-        load_chunks(3, [2])
+        load_samples(0, [FILLER])
+        load_samples(1, [FILLER])
+        load_b1(1, 0)
+        load_samples(2, [FILLER])
         load_b1(0, 1)
+        load_samples(3, inter_chunks)
         load_b1(1, 1)
-        load_chunks(4, [0, 1])
-        load_chunks(4, [2])
+        load_samples(3, [FILLER])
+        load_samples(4, inter_chunks)
+        load_samples(4, [FILLER])
+        e0_runs = load_vector("e0_runs", e0)
         load_w()
         for i in range(5, TILES):
-            load_chunks(i, [0, 1])
-            load_chunks(i, [2])
+            load_samples(i, inter_chunks)
+            load_samples(i, [FILLER])
 
-        if WARM:
-            warm(WARM)
-        sort_tile(0, [0, 1])
-        turn_run([(0, 0), (0, 1)], [])
-        spread_gain()
-        spread_e0()
-        if WARM:
-            warm(WARM)
-        sort_tile(1, [0, 1])
-        turn_run([(1, 0), (1, 1)], [])
-        sort_tile(2, [0, 1])
-        mm_inter(0, 0, 0)
-        turn_run([(2, 0), (2, 1)], [], lambda: b1_interleave(0, 0, False))
-        sort_words(0, 2, True)
-        mm_inter(1, 0, 1)
-        turn_run([(0, 2)], [], lambda: b1_quantise(0, 0))
-        b1_interleave(1, 0, False)
-        sort_words(1, 2, True)
-        mm_inter(2, 0, 2)
-        sort_words(3, 0, True)
-        sort_words(3, 1, False)
-        b1_quantise(1, 0)
-        turn_run([(1, 2), (3, 0), (3, 1)], [])
-        mm_filler(0, 0)
-        mm_filler(1, 0)
-        sort_words(2, 2, False)
-        sort_words(3, 2, False)
-        square_gain(0, 0)
-        square_gain(1, 0)
-        mm_inter(3, 0, 3)
-        turn_run([(2, 2), (3, 2)], [], lambda: b1_interleave(0, 1, False))
-        mm_inter(0, 1, 0)
-        mm_inter(1, 1, 1)
-        b1_quantise(0, 1)
-        b1_interleave(1, 1, False)
-        sort_words(4, 0, True)
-        sort_words(4, 1, True)
-        mm_filler(2, 0)
-        mm_filler(3, 0)
-        b1_quantise(1, 1)
-        sort_words(4, 2, False)
-        square_gain(2, 0)
-        square_gain(3, 0)
-        turn_run([(4, 0), (4, 1), (4, 2)], [[(0, 0), (1, 0)]])
-        mm_inter(2, 1, 2)
-        mm_filler(0, 1)
-        mm_filler(1, 1)
-        square_gain(0, 1)
-        square_gain(1, 1)
-        mm_inter(3, 1, 3)
-        mm_filler(2, 1)
-        mm_filler(3, 1)
-        sort_tile(5, [0, 1], ())
-        square_gain(2, 1)
-        square_gain(3, 1)
+        warm_up(WARM_FIRST)
+        sort_pairs(0, 0, on_vector)
+        turned = turn(chunk(6, 0, 0))
+        sort_pairs(1, 0, on_vector)
+        sort_pairs(2, 0, on_vector)
+        quantise_turned(turned)
+        warm_up(WARM_SECOND)
+        quantise_turned(turn(chunk(7, 1, 0), chunk(6, 2, 0)))
+        sort_pairs(0, 1, on_vector)
+        sort_pairs(1, 1, on_vector)
+        project_both(0, 0)
+        turned = turn(chunk(7, 0, 1))
+        sort_pairs(2, 1, on_vector)
+        quantise_turned(turned)
+        interleave_b1(0, 0)
+        project_both(1, 0)
+        turned = turn(chunk(6, 1, 1), chunk(7, 2, 1))
+        quantise_b1(0, 0)
+        quantise_turned(turned)
+        sort_pairs(0, FILLER, on_vector)
+        sort_pairs(1, FILLER, on_scalar)
+        project_both(2, 0)
+        project_both(0, 1)
+        interleave_b1(1, 0)
+        turned = turn(chunk(6, 0, FILLER), chunk(7, 1, FILLER))
+        sort_pairs(2, FILLER, on_scalar)
+        quantise_turned(turned[:1])
+        quantise_b1(1, 0)
+        quantise_turned(turned[1:])
+        project_both(1, 1)
+        turned = turn(chunk(6, 2, FILLER))
+        spread_gain(7)
+        interleave_b1(0, 1)
+        quantise_turned(turned)
+        sort_pairs(3, 0, on_scalar)
+        sort_pairs(3, 1, on_scalar)
+        quantise_b1(0, 1)
+        interleave_b1(1, 1)
+        project_both(2, 1)
 
-        mm_unit(4, 0, 0)
-        turn_run([(5, 0), (5, 1)], [[(0, 1), (1, 1)], [(2, 0), (3, 0)]])
-        sort_words(5, 2, False)
-        square_gain(4, 0)
-        mm_unit(4, 1, 1)
-        mm_out(0, 2)
-        mm_out(1, 3)
-        turn_run([(5, 2)], [[(2, 1), (3, 1)]], lambda: finish(0))
+        project(0, 0, [FILLER])
+        square_and_gain(0, 0)
+        quantise_turned(turn(chunk(6, 3, 0), chunk(7, 3, 1)))
+        quantise_b1(1, 1)
+        for i in (1, 2):
+            project(i, 0, [FILLER])
+            square_and_gain(i, 0)
+        sort_pairs(3, FILLER, on_scalar)
+        for i in head:
+            project(i, 1, [FILLER], passes=(0,))
+        project(3, 0, inter_chunks, bank=0)
+        turned = turn(chunk(6, 3, FILLER), halves(7, (0, 0), (1, 0)))
+        for c in all_chunks:
+            sort_pairs(4, c, on_vector)
+        quantise_turned(turned)
+        for i in head:
+            project(i, 1, [FILLER], passes=(1,))
+            square_and_gain(i, 1)
+        project(3, 1, inter_chunks, bank=2)
+        project(3, 0, [FILLER])
+
+        turned = turn(chunk(4, 4, 0), chunk(6, 4, 1), chunk(7, 4, FILLER), halves(1, (0, 1), (1, 1)))
+        spread_e0(3)
+        quantise_turned(turned)
+        project(3, 1, [FILLER])
+        for c in all_chunks:
+            sort_pairs(5, c, on_vector)
+        square_and_gain(3, 0)
+        square_and_gain(3, 1)
+        project(4, 0, all_chunks, bank=5)
+        modulus(0, 0)
+        modulus(1, 2)
+        square_and_gain(4, 0)
+        turned = turn(
+            chunk(1, 5, 0), chunk(4, 5, 1), chunk(6, 5, FILLER), halves(7, (2, 0), (2, 1)), halves(3, (3, 0), (3, 1))
+        )
+        finish(0)
         finish(1)
-        square_gain(4, 1)
-        sort_tile(6, [0, 1, 2], SC)
+        quantise_turned(turned)
+        project(4, 1, all_chunks, bank=5)
+        modulus(2, 2)
+
+        last = TILES - 1
         for i in range(5, TILES):
-            mm_unit(i, 0, 0)
+            ahead = all_chunks if i < last else []
+            for c in ahead:
+                sort_pairs(i + 1, c, on_scalar if c == FILLER else on_vector)
+            square_and_gain(i - 1, 1)
             if i == 5:
-                mm_out(2, 2)
-                mm_out(3, 3)
                 finish(2)
-            else:
-                mm_out(i - 2, 2 + i % 2)
-            square_gain(i, 0)
-            turn_run([(i + 1, c) for c in range(3)] if i + 1 < TILES else [], [both(i - 1)], lambda: finish(i - 2))
-            mm_unit(i, 1, 1)
-            if i + 2 < TILES:
-                sort_tile(i + 2, [0, 1, 2], SC)
-            square_gain(i, 1, 2 if i == 7 else 1)
-        turn_run([], [[(7, 0)]])
-        mm_out(6, 2)
-        mm_out(7, 0, (0,))
-        turn_run([], [[(7, 1)]], lambda: finish(6))
-        mm_out(7, 0, (1,))
-        finish(7, 2)
+            project(i, 0, all_chunks, bank=0)
+            modulus(i - 2, 2 + i % 2)
+            square_and_gain(i, 0)
+            turned = turn(*[chunk(4 + c, i + 1, c) for c in ahead], halves(7, (i - 1, 0), (i - 1, 1)))
+            finish(i - 2)
+            quantise_turned(turned)
+            project(i, 1, all_chunks, bank=1)
+
+        square_and_gain(last, 1, pieces=2)
+        turned = turn(halves(4, (last, 0)))
+        modulus(last - 1, 2)
+        quantise_turned(turned)
+        turned = turn(halves(5, (last, 1)))
+        finish(last - 1)
+        quantise_turned(turned)
+        modulus(last, 0)
+        finish(last, pieces=2)

from contextlib import ExitStack

import concourse.mybir as mybir
from concourse.masks import make_identity

M, KF, KI, F, R = 1024, 1024, 2048, 1024, 512
FLOPS = 2 * M * (KF + KI) * F + 2 * M * F * R

F32 = mybir.dt.float32
BF16 = mybir.dt.bfloat16
I32 = mybir.dt.int32
U32 = mybir.dt.uint32
U8 = mybir.dt.uint8
FP8X4 = mybir.dt.float8_e4m3fn_x4
FP4X4 = mybir.dt.float4_e2m1fn_x4
SQUARE = mybir.ActivationFunctionType.Square
ALU = mybir.AluOpType

P = 128
PASS = 512
HALF = 512
CHUNK = 2 * PASS
FILLER = 2
TILES = M // P
HEAD = 3
WARM_FIRST, WARM_SECOND = 10, 6


def tile_squared_projection_modulus_s3_kernel(
    tc, filler, inter, b1, b2_words, b2_scales, gain, w_words, w_scales, e0, out
):
    nc = tc.nc
    with ExitStack() as ctx:
        keep = ctx.enter_context(tc.tile_pool(name="keep", bufs=1))
        work = ctx.enter_context(tc.tile_pool(name="work", bufs=4))
        psum = ctx.enter_context(tc.psum_pool(name="psum", bufs=1))
        ctx.enter_context(tc.manual_schedule())

        raw = {}
        pairs = {}
        stationary = {}
        moving = {}
        b1_stage = {}
        sums = {}

        def bank_tile(bank, shape):
            return psum.tile(shape, F32, name="bank_%d" % bank)

        def load_samples(i, chunks):
            staged = keep.tile([P, CHUNK * len(chunks)], BF16, name="raw_%d_%d" % (i, chunks[0]))
            rows = slice(P * i, P * (i + 1))
            if chunks[0] == FILLER:
                source = filler[rows, :]
            else:
                source = inter[rows, CHUNK * chunks[0] : CHUNK * (chunks[-1] + 1)]
            nc.sync.dma_start(out=staged[:], in_=source)
            for n, c in enumerate(chunks):
                raw[i, c] = staged[:, CHUNK * n : CHUNK * (n + 1)].bitcast(F32)

        def new_plane(name, width):
            plane = keep.tile([P, 2, width], U8, name=name, align_bytes=64)
            nc.vector.memset(plane[:].bitcast(U32), 0)
            return plane

        def load_fp4(name, words, scales, plane):
            for q in range(4):
                rows = scales[:, 4 * q : 4 * q + 4, :].rearrange("g r n -> r g n")
                nc.sync.dma_start(out=plane[32 * q : 32 * q + 4, :, :].bitcast(I32), in_=rows.bitcast(I32))
            codes = keep.tile([P, 2, words.shape[2]], U8, name=name, align_bytes=64)
            nc.sync.dma_start(out=codes[:].bitcast(I32), in_=words.rearrange("g p n -> p g n").bitcast(I32))
            return codes

        def load_b2(c):
            passes = slice(2 * c, 2 * c + 2)
            codes = load_fp4("b2_%d" % c, b2_words[passes], b2_scales[passes], b2_planes[c])
            for g in range(2):
                for h in range(2):
                    moving[c, g, h] = (
                        codes[:, g, 2 * HALF * h : 2 * HALF * (h + 1)].bitcast(FP4X4),
                        b2_planes[c][:, g, HALF * h : HALF * (h + 1)],
                    )

        def load_w():
            codes = load_fp4("w", w_words, w_scales, w_plane)
            for h in range(2):
                moving["w", h] = (codes[:, h, :].bitcast(FP4X4), w_plane[:, h, :])

        def load_b1(g, h):
            staged = keep.tile([P, 4, HALF], BF16, name="b1_rows_%d_%d" % (g, h))
            rows = b1[PASS * g : PASS * (g + 1), HALF * h : HALF * (h + 1)]
            nc.sync.dma_start(out=staged[:], in_=rows.rearrange("(p t) n -> p t n", t=4))
            b1_stage[g, h] = staged

        def load_vector(name, vector):
            run = vector.shape[0] // P
            staged = keep.tile([P, run], BF16, name=name)
            nc.sync.dma_start(out=staged[:], in_=vector.rearrange("(p j) -> p j", j=run))
            return staged

        def quantise(name, values):
            width = values.shape[1] // 4
            words = keep.tile([P, width], U32, name=name + "_words", align_bytes=64)
            plane = keep.tile([P, width], U8, name=name + "_plane", align_bytes=64)
            nc.vector.quantize_mx(out=words[:].bitcast(FP8X4), scales=plane[:], in_=values)
            return words, plane

        def interleave_b1(g, h):
            grouped = work.tile([P, HALF, 4], BF16, name="b1_grouped", bufs=2, align_bytes=64)
            nc.vector.tensor_copy(
                out=grouped[:].rearrange("p (c i) t -> p c t i", i=4),
                in_=b1_stage[g, h][:].rearrange("p t (c i) -> p c t i", i=4),
            )
            b1_stage[g, h] = grouped

        def quantise_b1(g, h):
            words, plane = quantise("b1_%d_%d" % (g, h), b1_stage[g, h][:].rearrange("p n t -> p (n t)"))
            moving[FILLER, g, h] = (words[:].bitcast(FP8X4), plane[:])

        def sort_pairs(i, c, copy):
            sorted_pairs = work.tile([P, 2, 2, P], F32, name="sorted_pairs", bufs=6)
            copy(
                out=sorted_pairs[:].rearrange("s u g (b i) -> s (g b) u i", i=4),
                in_=raw[i, c].rearrange("s (b i u) -> s b u i", i=4, u=2),
            )
            pairs[i, c] = sorted_pairs[:].rearrange("s u g p -> s g u p")

        def turn(*jobs):
            turned = []
            banks = []
            for bank, passes in jobs:
                tile = bank_tile(bank, [P, 2, 2, P])
                for n, (key, g) in enumerate(passes):
                    for u in range(2):
                        nc.tensor.transpose(tile[:, n, u, :], pairs[key][:, g, u, :], identity[:])
                banks.append(tile)
            for (bank, passes), tile in zip(jobs, banks):
                values = work.tile([P, len(passes) * PASS], BF16, name="turned", bufs=6, align_bytes=64)
                nc.scalar.copy(
                    out=values[:].bitcast(F32).rearrange("p (n s u) -> p n s u", n=len(passes), u=2),
                    in_=tile[:, 0 : len(passes), :, :].rearrange("p n u s -> p n s u"),
                )
                turned.append((passes, values))
            return turned

        def quantise_turned(turned):
            for passes, values in turned:
                name = "_".join(str(part) for part in passes[0][0])
                words, plane = quantise("x_" + name, values[:])
                for n, (key, g) in enumerate(passes):
                    stationary[key, g] = (words[:, P * n : P * (n + 1)], plane[:, P * n : P * (n + 1)])

        def chunk(bank, i, c):
            return bank, [((i, c), 0), ((i, c), 1)]

        def halves(bank, *units):
            return bank, [((i, "h", h), 0) for i, h in units]

        def spread(bank, staged, write, read):
            words = staged[:].bitcast(F32)
            count = words.shape[1]
            tile = bank_tile(bank, [P, count, P])
            for n in range(count):
                nc.tensor.transpose(tile[:, n, :], words[:, n : n + 1].to_broadcast([P, P]), identity[:])
            nc.scalar.copy(out=write, in_=read(tile[:]))

        def spread_gain(bank):
            spread(
                bank, gain_runs,
                gain_rows[:].bitcast(F32).rearrange("s (h u j v) -> s h u j v", h=2, u=2, v=2),
                lambda tile: tile.rearrange("s (v u) (h j) -> s h u j v", u=2, h=2),
            )

        def spread_e0(bank):
            spread(
                bank, e0_runs,
                e0_rows[:].bitcast(F32).rearrange("s (j n) -> s j n", n=2),
                lambda tile: tile.rearrange("s n j -> s j n"),
            )

        def mx_pass(result, lhs, rhs, start, stop):
            nc.tensor.matmul_mx(
                out=result, lhsT=lhs[0].bitcast(FP8X4), lhsT_scale=lhs[1], rhs=rhs[0], rhs_scale=rhs[1],
                start=start, stop=stop,
            )

        def project(i, h, chunks, bank=None, passes=(0, 1)):
            if bank is not None:
                sums[i, h] = bank_tile(bank, [P, HALF])
            for c in chunks:
                for g in passes:
                    first, last = (c, g) == (0, 0), (c, g) == (FILLER, 1)
                    mx_pass(sums[i, h][:], stationary[(i, c), g], moving[c, g, h], first, last)

        def project_both(i, c):
            for h in range(2):
                project(i, h, [c], bank=2 * i + h if c == 0 else None)

        def square_and_gain(i, h, pieces=1):
            rounded = work.tile([P, HALF], BF16, name="rounded", bufs=8)
            source = sums[i, h][:].rearrange("s (p u e) -> s u p e", u=2, e=2)
            step = 2 // pieces
            for u in range(0, 2, step):
                squares = work.tile([P, step, P, 2], F32, name="squares")
                nc.scalar.activation(out=squares[:], in_=source[:, u : u + step, :, :], func=SQUARE)
                first, width = 2 * P * u, 2 * P * step
                nc.vector.tensor_tensor(
                    out=rounded[:, first : first + width],
                    in0=squares[:].rearrange("s u p e -> s (u p e)"),
                    in1=gain_rows[:, HALF * h + first : HALF * h + first + width],
                    op=ALU.mult,
                )
            pairs[i, "h", h] = rounded[:].bitcast(F32).rearrange("s (g u p) -> s g u p", g=1, u=2)

        def modulus(i, bank):
            sums[i] = bank_tile(bank, [P, R])
            for h in range(2):
                mx_pass(sums[i][:], stationary[(i, "h", h), 0], moving["w", h], h == 0, h == 1)

        def finish(i, pieces=1):
            width = R // pieces
            for n in range(pieces):
                cols = slice(width * n, width * (n + 1))
                result = work.tile([P, width], F32, name="result")
                nc.vector.tensor_tensor(out=result[:], in0=sums[i][:, cols], in1=e0_rows[:, cols], op=ALU.add)
                nc.sync.dma_start(out=out[P * i : P * (i + 1), cols], in_=result[:])

        def warm_up(passes):
            tile = bank_tile(5, [P, 4, P])
            for n in range(passes):
                mx_pass(tile[:, n % 4, :], warm, (warm[0].bitcast(FP8X4), warm[1]), True, True)

        on_vector, on_scalar = nc.vector.tensor_copy, nc.scalar.copy
        inter_chunks = [0, 1]
        all_chunks = [0, 1, FILLER]

        identity = keep.tile([P, P], F32, name="identity")
        make_identity(nc, identity[:])
        gain_rows = keep.tile([P, F], BF16, name="gain_rows")
        e0_rows = keep.tile([P, R], BF16, name="e0_rows")

        b2_planes = [new_plane("b2_plane_0", F)]
        ones = keep.tile([P, PASS], BF16, name="ones", align_bytes=64)
        nc.vector.memset(ones[:], 1.0)
        warm_words, warm_plane = quantise("warm", ones[:])
        warm = (warm_words[:], warm_plane[:])
        b2_planes.append(new_plane("b2_plane_1", F))
        w_plane = new_plane("w_plane", R)
        table_warm = keep.tile([P, 1], F32, name="table_warm")
        nc.scalar.activation(out=table_warm[:], in_=identity[:, 0:1], func=SQUARE)

        head = range(HEAD)
        for i in head:
            load_samples(i, [0])
        load_b2(0)
        for i in head:
            load_samples(i, [1])
        load_b1(0, 0)
        gain_runs = load_vector("gain_runs", gain)
        load_b2(1)
        load_samples(0, [FILLER])
        load_samples(1, [FILLER])
        load_b1(1, 0)
        load_samples(2, [FILLER])
        load_b1(0, 1)
        load_samples(3, inter_chunks)
        load_b1(1, 1)
        load_samples(3, [FILLER])
        load_samples(4, inter_chunks)
        load_samples(4, [FILLER])
        e0_runs = load_vector("e0_runs", e0)
        load_w()
        for i in range(5, TILES):
            load_samples(i, inter_chunks)
            load_samples(i, [FILLER])

        warm_up(WARM_FIRST)
        sort_pairs(0, 0, on_vector)
        turned = turn(chunk(6, 0, 0))
        sort_pairs(1, 0, on_vector)
        sort_pairs(2, 0, on_vector)
        quantise_turned(turned)
        warm_up(WARM_SECOND)
        quantise_turned(turn(chunk(7, 1, 0), chunk(6, 2, 0)))
        sort_pairs(0, 1, on_vector)
        sort_pairs(1, 1, on_vector)
        project_both(0, 0)
        turned = turn(chunk(7, 0, 1))
        sort_pairs(2, 1, on_vector)
        quantise_turned(turned)
        interleave_b1(0, 0)
        project_both(1, 0)
        turned = turn(chunk(6, 1, 1), chunk(7, 2, 1))
        quantise_b1(0, 0)
        quantise_turned(turned)
        sort_pairs(0, FILLER, on_vector)
        sort_pairs(1, FILLER, on_scalar)
        project_both(2, 0)
        project_both(0, 1)
        interleave_b1(1, 0)
        turned = turn(chunk(6, 0, FILLER), chunk(7, 1, FILLER))
        sort_pairs(2, FILLER, on_scalar)
        quantise_turned(turned[:1])
        quantise_b1(1, 0)
        quantise_turned(turned[1:])
        project_both(1, 1)
        turned = turn(chunk(6, 2, FILLER))
        spread_gain(7)
        interleave_b1(0, 1)
        quantise_turned(turned)
        sort_pairs(3, 0, on_scalar)
        sort_pairs(3, 1, on_scalar)
        quantise_b1(0, 1)
        interleave_b1(1, 1)
        project_both(2, 1)

        project(0, 0, [FILLER])
        square_and_gain(0, 0)
        quantise_turned(turn(chunk(6, 3, 0), chunk(7, 3, 1)))
        quantise_b1(1, 1)
        for i in (1, 2):
            project(i, 0, [FILLER])
            square_and_gain(i, 0)
        sort_pairs(3, FILLER, on_scalar)
        for i in head:
            project(i, 1, [FILLER], passes=(0,))
        project(3, 0, inter_chunks, bank=0)
        turned = turn(chunk(6, 3, FILLER), halves(7, (0, 0), (1, 0)))
        for c in all_chunks:
            sort_pairs(4, c, on_vector)
        quantise_turned(turned)
        for i in head:
            project(i, 1, [FILLER], passes=(1,))
            square_and_gain(i, 1)
        project(3, 1, inter_chunks, bank=2)
        project(3, 0, [FILLER])

        turned = turn(chunk(4, 4, 0), chunk(6, 4, 1), chunk(7, 4, FILLER), halves(1, (0, 1), (1, 1)))
        spread_e0(3)
        quantise_turned(turned)
        project(3, 1, [FILLER])
        for c in all_chunks:
            sort_pairs(5, c, on_vector)
        square_and_gain(3, 0)
        square_and_gain(3, 1)
        project(4, 0, all_chunks, bank=5)
        modulus(0, 0)
        modulus(1, 2)
        square_and_gain(4, 0)
        turned = turn(
            chunk(1, 5, 0), chunk(4, 5, 1), chunk(6, 5, FILLER), halves(7, (2, 0), (2, 1)), halves(3, (3, 0), (3, 1))
        )
        finish(0)
        finish(1)
        quantise_turned(turned)
        project(4, 1, all_chunks, bank=5)
        modulus(2, 2)

        last = TILES - 1
        for i in range(5, TILES):
            ahead = all_chunks if i < last else []
            for c in ahead:
                sort_pairs(i + 1, c, on_scalar if c == FILLER else on_vector)
            square_and_gain(i - 1, 1)
            if i == 5:
                finish(2)
            project(i, 0, all_chunks, bank=0)
            modulus(i - 2, 2 + i % 2)
            square_and_gain(i, 0)
            turned = turn(*[chunk(4 + c, i + 1, c) for c in ahead], halves(7, (i - 1, 0), (i - 1, 1)))
            finish(i - 2)
            quantise_turned(turned)
            project(i, 1, all_chunks, bank=1)

        square_and_gain(last, 1, pieces=2)
        turned = turn(halves(4, (last, 0)))
        modulus(last - 1, 2)
        quantise_turned(turned)
        turned = turn(halves(5, (last, 1)))
        finish(last - 1)
        quantise_turned(turned)
        modulus(last, 0)
        finish(last, pieces=2)
